import numpy as np
import ml_dtypes


def mxq(x, axis, fmt="e4m3"):
    dtype, down = {"e4m3": (ml_dtypes.float8_e4m3fn, 7), "e5m2": (ml_dtypes.float8_e5m2, 14)}[fmt]
    v = np.moveaxis(np.asarray(x, np.float32).astype(ml_dtypes.bfloat16).astype(np.float64), axis, -1)
    blocks = v.reshape(v.shape[:-1] + (-1, 32))
    amax = np.abs(blocks).max(-1, keepdims=True)
    byte = np.maximum(np.where(amax > 0, np.frexp(amax)[1] - 1 + 127, 0) - down, 1)
    scale = np.exp2(byte - 127.0)
    codes = (blocks / scale).astype(np.float32).astype(dtype).astype(np.float64)
    return np.moveaxis((codes * scale).reshape(v.shape), -1, axis)


WIDE = False


def mx_kscale(k):
    if not WIDE:
        return np.ones(k)
    levels = np.array([10, -10, 5, -5, 0])
    if k % 512:
        return np.exp2(np.random.permutation(np.resize(levels, k // 32))).repeat(32)
    a = np.empty((k // 512, 16))
    for p in range(k // 512):
        a[p, :8] = np.random.permutation(np.resize(levels, 8))
        for g in range(8):
            far = levels[np.abs(levels - a[p, g]) >= 10]
            a[p, g + 8] = far[np.random.randint(len(far))]
    return np.exp2(a.ravel()).repeat(32)


def f64(x):
    return np.asarray(x).astype(np.float64)


def striped(idx):
    return np.tile(idx.reshape(-1, 16).T, (8, 1)).astype(np.uint16)


def unstriped(offs):
    return offs[:16].T.reshape(-1).astype(np.int64)


K, T, E, C, N = 2048, 1280, 6, 128, 128


def by_expert(wq, xq):
    return np.concatenate([wq[e].T @ xq[:, e * C:(e + 1) * C] for e in range(E)], axis=1)


def setup_inputs():
    n = np.random.standard_normal
    s = mx_kscale(K)[:, None]
    return {
        "xT": (n((K, T)) * s).astype(np.float32),
        "w": (n((E + 1, K, N)) / np.sqrt(K) / s[None]).astype(np.float32),
        "gate": np.tile(np.random.uniform(0.2, 1.0, E * C), (N, 1)).astype(np.float32),
        "offs": striped(np.random.permutation(T)[:E * C]),
    }


def reference(xT, w, gate, offs):
    idx = unstriped(offs)
    wq = mxq(f64(w), 1, "e4m3")
    xs = mxq(f64(xT), 0, "e4m3")
    ys = wq[E].T @ xs
    xq = mxq(f64(xT)[:, idx], 0, "e4m3")
    y = by_expert(wq, xq)
    out = ys
    out[:, idx] += f64(gate) * y
    return out

@@ -1,0 +1,238 @@
+from contextlib import ExitStack
+
+import concourse.mybir as mybir
+
+K, T, E, C, N = 2048, 1280, 6, 128, 128
+S = E * C
+
+FLOPS = 2 * K * N * (S + T)
+
+F32 = mybir.dt.float32
+BF16 = mybir.dt.bfloat16
+U32 = mybir.dt.uint32
+U16 = mybir.dt.uint16
+U8 = mybir.dt.uint8
+FP8X4 = mybir.dt.float8_e4m3fn_x4
+ADD = mybir.AluOpType.add
+MULT = mybir.AluOpType.mult
+
+P = 128
+KP = 512
+G = K // KP
+BANKS = ((0, 512), (512, 1024), (1024, 1280))
+
+
+def tile_moe_shr_lin_none_kernel(tc, xT, w, gate, offs, out):
+    nc = tc.nc
+    with ExitStack() as ctx:
+        keep = ctx.enter_context(tc.tile_pool(name="keep", bufs=1))
+        xraw_pool = ctx.enter_context(tc.tile_pool(name="xraw", bufs=4))
+        wraw_pool = ctx.enter_context(tc.tile_pool(name="wraw", bufs=3))
+        pair_pool = ctx.enter_context(tc.tile_pool(name="pairs", bufs=3))
+        ring = ctx.enter_context(tc.tile_pool(name="ring", bufs=2))
+        quad_pool = ctx.enter_context(tc.tile_pool(name="quadp", bufs=3))
+        wring = ctx.enter_context(tc.tile_pool(name="wring", bufs=4))
+        psum = ctx.enter_context(tc.psum_pool(name="psum", bufs=1))
+
+        offsets = keep.tile([P, S // 16], U16, name="offsets")
+        nc.sync.dma_start(offsets[:], offs)
+
+        xc = keep.tile([P, G, T], U32, name="xc", align_bytes=64)
+        xs = keep.tile([P, G, T], U8, name="xs", align_bytes=64)
+        gc = keep.tile([P, G, S], U32, name="gc", align_bytes=64)
+        gs = keep.tile([P, G, S], U8, name="gs", align_bytes=64)
+        wc = keep.tile([P, E + 1, KP], U32, name="wc", align_bytes=64)
+        ws = keep.tile([P, E + 1, KP], U8, name="ws", align_bytes=64)
+        window = keep.tile([P, T], F32, name="window")
+        result = keep.tile([P, T], F32, name="result")
+        gates = keep.tile([P, S], F32, name="gates")
+        y = keep.tile([P, S], F32, name="y")
+        nc.gpsimd.memset(window[:], 0.0)
+
+        shared = [psum.tile([P, b - a], F32, name=f"shared{a}") for a, b in BANKS]
+        routed = [psum.tile([P, 512], F32, name="routed0"), psum.tile([P, 256], F32, name="routed1")]
+
+        raws, pairs, wraws, wquads = {}, {}, {}, {}
+
+        def load_x(g, u, cuts=(0, T)):
+            raw = xraw_pool.tile([P, 2, T], F32, name="xraw")
+            src = xT[g * KP : (g + 1) * KP, :].rearrange("(p u e) t -> p u e t", u=2, e=2)
+            for a, b in zip(cuts[:-1], cuts[1:]):
+                nc.sync.dma_start(raw[:, :, a:b], src[:, u, :, a:b])
+            raws[g, u] = raw
+
+        def load_w(e, cuts=(0, G)):
+            raw = wraw_pool.tile([P, G, KP], F32, name="wraw")
+            src = w[e].rearrange("(g p j) n -> p g (j n)", p=P, j=4)
+            for a, b in zip(cuts[:-1], cuts[1:]):
+                nc.sync.dma_start(raw[:, a:b, :], src[:, a:b, :])
+            wraws[e] = raw
+
+        def cast_x(engine_copy, g, u, a=0, b=T):
+            if g not in pairs:
+                pairs[g] = pair_pool.tile([P, 2, 2 * T], BF16, name="pairs", align_bytes=64)
+            engine_copy(
+                out=pairs[g][:, u, :].rearrange("p (t e) -> p t e", e=2)[:, a:b, :],
+                in_=raws[g, u][:, :, a:b].rearrange("p e t -> p t e"),
+            )
+
+        def cast_w(engine_copy, e, a=0, b=G):
+            if e not in wquads:
+                wquads[e] = wring.tile([P, G, KP], BF16, name="wquad", align_bytes=64)
+            engine_copy(
+                out=wquads[e][:, a:b, :].rearrange("p g (n j) -> p g n j", j=4),
+                in_=wraws[e][:, a:b, :].rearrange("p g (j n) -> p g n j", j=4),
+            )
+
+        def quant_w(e, a=0, b=G):
+            nc.vector.quantize_mx(
+                out=wc[:, e, a * N : b * N].bitcast(FP8X4),
+                scales=ws[:, e, a * N : b * N],
+                in_=wquads[e][:, a:b, :].rearrange("p g c -> p (g c)"),
+            )
+
+        gp, gq, quads = {}, {}, {}
+
+        def gather(g, u):
+            if g not in gp:
+                gp[g] = ring.tile([P, 2, 2 * S], BF16, name="gp", align_bytes=64)
+            nc.vector.tensor_copy(gp[g][:, u, :].bitcast(U32), pairs[g][:, u, :].bitcast(U32).indirect(offsets[:]))
+
+        def weave_tokens(engine_copy, g):
+            quads[g] = quad_pool.tile([P, 4 * T], BF16, name="quads", align_bytes=64)
+            engine_copy(
+                out=quads[g][:].rearrange("p (t u e) -> p t u e", u=2, e=2),
+                in_=pairs[g][:].rearrange("p u (t e) -> p t u e", e=2),
+            )
+
+        def weave_slots(engine_copy, g):
+            gq[g] = ring.tile([P, 4 * S], BF16, name="gq", align_bytes=64)
+            engine_copy(
+                out=gq[g][:].rearrange("p (s u e) -> p s u e", u=2, e=2),
+                in_=gp[g][:].rearrange("p u (s e) -> p s u e", e=2),
+            )
+
+        def quant_tokens(g):
+            for a, b in ((0, 1024), (1024, 1280)):
+                nc.vector.quantize_mx(out=xc[:, g, a:b].bitcast(FP8X4), scales=xs[:, g, a:b], in_=quads[g][:, 4 * a : 4 * b])
+
+        def quant_slots(g):
+            for a, b in ((0, 512), (512, 768)):
+                nc.vector.quantize_mx(out=gc[:, g, a:b].bitcast(FP8X4), scales=gs[:, g, a:b], in_=gq[g][:, 4 * a : 4 * b])
+
+        def mm_shared(g):
+            for bank, (a, b) in zip(shared, BANKS):
+                nc.tensor.matmul_mx(
+                    out=bank[:],
+                    lhsT=wc[:, E, g * N : (g + 1) * N].bitcast(FP8X4),
+                    lhsT_scale=ws[:, E, g * N : (g + 1) * N],
+                    rhs=xc[:, g, a:b].bitcast(FP8X4),
+                    rhs_scale=xs[:, g, a:b],
+                    start=(g == 0),
+                    stop=(g == G - 1),
+                )
+
+        def mm_routed(e):
+            bank = routed[e // 4][:, (e % 4) * C : (e % 4 + 1) * C]
+            for g in range(G):
+                nc.tensor.matmul_mx(
+                    out=bank,
+                    lhsT=wc[:, e, g * N : (g + 1) * N].bitcast(FP8X4),
+                    lhsT_scale=ws[:, e, g * N : (g + 1) * N],
+                    rhs=gc[:, g, e * C : (e + 1) * C].bitcast(FP8X4),
+                    rhs_scale=gs[:, g, e * C : (e + 1) * C],
+                    start=(g == 0),
+                    stop=(g == G - 1),
+                )
+            nc.scalar.copy(out=y[:, e * C : (e + 1) * C], in_=bank)
+
+        def scatter(a, b):
+            nc.vector.tensor_tensor(
+                window[:].indirect(offsets[:, a // 16 : b // 16]), y[:, a:b], gates[:, a:b], MULT
+            )
+
+        V, A = nc.vector.tensor_copy, nc.scalar.copy
+        H = T // 2
+
+        load_w(E, (0, 2, 4))
+        load_x(0, 0, (0, H, T))
+        load_x(0, 1, (0, H, T))
+        load_x(1, 0)
+        load_x(1, 1)
+
+        cast_w(V, E, 0, 2)
+        cast_w(V, E, 2, 4)
+        quant_w(E, 0, 2)
+        cast_x(A, 0, 0, 0, H)
+        quant_w(E, 2, 4)
+        cast_x(V, 0, 0, H, T)
+        cast_x(A, 0, 1, 0, H)
+        gather(0, 0)
+        cast_x(V, 0, 1, H, T)
+        load_x(2, 0)
+        cast_x(A, 1, 0)
+        gather(0, 1)
+        weave_tokens(V, 0)
+        weave_slots(V, 0)
+        load_x(2, 1)
+        cast_x(A, 1, 1)
+        gather(1, 0)
+        quant_tokens(0)
+        quant_slots(0)
+        mm_shared(0)
+        gather(1, 1)
+        load_x(3, 0)
+        cast_x(A, 2, 0)
+        weave_tokens(V, 1)
+        weave_slots(V, 1)
+        load_x(3, 1)
+        cast_x(A, 2, 1)
+        load_w(0)
+        gather(2, 0)
+        quant_tokens(1)
+        quant_slots(1)
+        mm_shared(1)
+        gather(2, 1)
+        load_w(1)
+        nc.sync.dma_start(gates[:], gate)
+        cast_x(A, 3, 0)
+        load_w(2)
+        cast_x(A, 3, 1)
+        weave_tokens(A, 2)
+        weave_slots(V, 2)
+        gather(3, 0)
+        cast_w(A, 0)
+        load_w(3)
+        gather(3, 1)
+        quant_tokens(2)
+        quant_slots(2)
+        mm_shared(2)
+        weave_tokens(A, 3)
+        weave_slots(V, 3)
+        quant_w(0)
+        cast_w(A, 1)
+        load_w(4)
+        quant_slots(3)
+        mm_routed(0)
+        cast_w(A, 2)
+        load_w(5)
+        quant_w(1)
+        quant_tokens(3)
+        mm_shared(3)
+        mm_routed(1)
+        cast_w(A, 3)
+        quant_w(2)
+        mm_routed(2)
+        cast_w(A, 4)
+        quant_w(3)
+        mm_routed(3)
+        cast_w(A, 5)
+        scatter(0, 512)
+        quant_w(4)
+        mm_routed(4)
+        quant_w(5)
+        mm_routed(5)
+        scatter(512, 768)
+        for bank, (a, b) in zip(shared, BANKS):
+            nc.vector.tensor_tensor(result[:, a:b], bank[:], window[:, a:b], ADD)
+            nc.sync.dma_start(out[:, a:b], result[:, a:b])

@@ -93,6 +93,12 @@ def tile_moe_shr_lin_none_kernel(tc, xT, w, gate, offs, out):
 
         gp, gq, quads = {}, {}, {}
 
+        def weave(engine_copy, dst, src):
+            engine_copy(
+                out=dst.bitcast(F32).rearrange("p (t u) -> p t u", u=2),
+                in_=src.bitcast(F32).rearrange("p u t -> p t u"),
+            )
+
         def gather(g, u):
             if g not in gp:
                 gp[g] = ring.tile([P, 2, 2 * S], BF16, name="gp", align_bytes=64)
@@ -100,17 +106,11 @@ def tile_moe_shr_lin_none_kernel(tc, xT, w, gate, offs, out):
 
         def weave_tokens(engine_copy, g):
             quads[g] = quad_pool.tile([P, 4 * T], BF16, name="quads", align_bytes=64)
-            engine_copy(
-                out=quads[g][:].rearrange("p (t u e) -> p t u e", u=2, e=2),
-                in_=pairs[g][:].rearrange("p u (t e) -> p t u e", e=2),
-            )
+            weave(engine_copy, quads[g][:], pairs[g][:])
 
         def weave_slots(engine_copy, g):
             gq[g] = ring.tile([P, 4 * S], BF16, name="gq", align_bytes=64)
-            engine_copy(
-                out=gq[g][:].rearrange("p (s u e) -> p s u e", u=2, e=2),
-                in_=gp[g][:].rearrange("p u (s e) -> p s u e", e=2),
-            )
+            weave(engine_copy, gq[g][:], gp[g][:])
 
         def quant_tokens(g):
             for a, b in ((0, 1024), (1024, 1280)):
@@ -144,7 +144,9 @@ def tile_moe_shr_lin_none_kernel(tc, xT, w, gate, offs, out):
                     start=(g == 0),
                     stop=(g == G - 1),
                 )
-            nc.scalar.copy(out=y[:, e * C : (e + 1) * C], in_=bank)
+
+        def ycopy(engine_copy, lo, hi):
+            engine_copy(out=y[:, lo * C : hi * C], in_=routed[lo // 4][:, 0 : (hi - lo) * C])
 
         def scatter(a, b):
             nc.vector.tensor_tensor(
@@ -152,87 +154,90 @@ def tile_moe_shr_lin_none_kernel(tc, xT, w, gate, offs, out):
             )
 
         V, A = nc.vector.tensor_copy, nc.scalar.copy
+
         H = T // 2
 
-        load_w(E, (0, 2, 4))
-        load_x(0, 0, (0, H, T))
-        load_x(0, 1, (0, H, T))
-        load_x(1, 0)
-        load_x(1, 1)
-
-        cast_w(V, E, 0, 2)
-        cast_w(V, E, 2, 4)
-        quant_w(E, 0, 2)
-        cast_x(A, 0, 0, 0, H)
-        quant_w(E, 2, 4)
-        cast_x(V, 0, 0, H, T)
-        cast_x(A, 0, 1, 0, H)
-        gather(0, 0)
-        cast_x(V, 0, 1, H, T)
-        load_x(2, 0)
-        cast_x(A, 1, 0)
-        gather(0, 1)
-        weave_tokens(V, 0)
-        weave_slots(V, 0)
-        load_x(2, 1)
-        cast_x(A, 1, 1)
-        gather(1, 0)
+        load_x(0,1,(0,384,768,1280))
+        load_x(0,0,(0,640,1280))
+        load_x(1,1)
+        cast_x(V,0,1)
+        cast_x(A,0,0,0,256)
+        load_x(1,0)
+        cast_x(A,0,0,768,1280)
+        gather(0,1)
+        cast_x(V,0,0,256,768)
+        weave_tokens(A,0)
+        gather(0,0)
+        cast_x(A,1,0)
+        load_x(3,0)
+        cast_x(A,3,0)
+        load_x(2,0)
+        weave_slots(V,0)
+        load_x(2,1)
+        cast_x(V,1,1,0,896)
+        load_w(6,(0,2,4))
         quant_tokens(0)
-        quant_slots(0)
-        mm_shared(0)
-        gather(1, 1)
-        load_x(3, 0)
-        cast_x(A, 2, 0)
-        weave_tokens(V, 1)
-        weave_slots(V, 1)
-        load_x(3, 1)
-        cast_x(A, 2, 1)
+        load_x(3,1)
         load_w(0)
-        gather(2, 0)
-        quant_tokens(1)
-        quant_slots(1)
-        mm_shared(1)
-        gather(2, 1)
+        cast_x(V,1,1,896,1280)
+        gather(1,1)
+        quant_slots(0)
         load_w(1)
-        nc.sync.dma_start(gates[:], gate)
-        cast_x(A, 3, 0)
+        gather(1,0)
         load_w(2)
-        cast_x(A, 3, 1)
-        weave_tokens(A, 2)
-        weave_slots(V, 2)
-        gather(3, 0)
-        cast_w(A, 0)
-        load_w(3)
-        gather(3, 1)
-        quant_tokens(2)
-        quant_slots(2)
-        mm_shared(2)
-        weave_tokens(A, 3)
-        weave_slots(V, 3)
-        quant_w(0)
-        cast_w(A, 1)
+        gather(3,0)
+        cast_x(A,2,0)
+        cast_x(A,2,1)
+        weave_tokens(V,1)
+        weave_slots(A,1)
+        quant_tokens(1)
+        weave_tokens(A,2)
+        cast_w(V,6,0,2)
+        cast_w(V,6,2,4)
+        quant_w(6,2,4)
+        gather(2,0)
+        quant_slots(1)
         load_w(4)
-        quant_slots(3)
-        mm_routed(0)
-        cast_w(A, 2)
-        load_w(5)
+        cast_x(A,3,1)
+        cast_w(V,0)
+        gather(2,1)
+        gather(3,1)
+        quant_w(6,0,2)
+        quant_w(0)
+        mm_shared(0)
+        cast_w(A,1)
+        mm_shared(1)
         quant_w(1)
+        cast_w(V,2)
+        load_w(5)
+        quant_tokens(2)
+        weave_slots(A,3)
+        quant_slots(3)
+        weave_tokens(A,3)
+        mm_shared(2)
+        nc.sync.dma_start(gates[:], gate)
+        cast_w(V,5)
         quant_tokens(3)
         mm_shared(3)
-        mm_routed(1)
-        cast_w(A, 3)
-        quant_w(2)
-        mm_routed(2)
-        cast_w(A, 4)
-        quant_w(3)
-        mm_routed(3)
-        cast_w(A, 5)
-        scatter(0, 512)
+        load_w(3)
+        cast_w(A,4)
+        weave_slots(A,2)
         quant_w(4)
-        mm_routed(4)
+        quant_slots(2)
         quant_w(5)
+        mm_routed(0)
+        mm_routed(4)
+        cast_w(A,3)
+        quant_w(2)
         mm_routed(5)
-        scatter(512, 768)
+        quant_w(3)
+        mm_routed(2)
+        ycopy(A,4,6)
+        mm_routed(1)
+        scatter(512,768)
+        mm_routed(3)
+        ycopy(A,0,4)
+        scatter(0,512)
         for bank, (a, b) in zip(shared, BANKS):
             nc.vector.tensor_tensor(result[:, a:b], bank[:], window[:, a:b], ADD)
             nc.sync.dma_start(out[:, a:b], result[:, a:b])

@@ -79,9 +79,15 @@ def tile_moe_shr_lin_none_kernel(tc, xT, w, gate, offs, out):
         def cast_w(engine_copy, e, a=0, b=G):
             if e not in wquads:
                 wquads[e] = wring.tile([P, G, KP], BF16, name="wquad", align_bytes=64)
+            if engine_copy is GP:
+                GP(
+                    wquads[e][:, a:b, :].rearrange("p g (n j) -> p g n j", j=4),
+                    wraws[e][:, a:b, :].rearrange("p g (j n) -> p g n j", j=4),
+                )
+                return
             engine_copy(
-                out=wquads[e][:, a:b, :].rearrange("p g (n j) -> p g n j", j=4),
-                in_=wraws[e][:, a:b, :].rearrange("p g (j n) -> p g n j", j=4),
+                out=wquads[e][:, a:b, :].rearrange("p g (c i j) -> p g c j i", i=4, j=4),
+                in_=wraws[e][:, a:b, :].rearrange("p g (j c i) -> p g c j i", i=4, j=4),
             )
 
         def quant_w(e, a=0, b=G):
@@ -155,89 +161,94 @@ def tile_moe_shr_lin_none_kernel(tc, xT, w, gate, offs, out):
 
         V, A = nc.vector.tensor_copy, nc.scalar.copy
 
+        def GP(out, in_):
+            nc.gpsimd.tensor_scalar(out, in_, 1.0, 0.0, MULT, ADD)
+
         H = T // 2
 
-        load_x(0,1,(0,384,768,1280))
-        load_x(0,0,(0,640,1280))
-        load_x(1,1)
+        load_x(0,1)
+        load_x(0,0)
         cast_x(V,0,1)
-        cast_x(A,0,0,0,256)
-        load_x(1,0)
-        cast_x(A,0,0,768,1280)
         gather(0,1)
-        cast_x(V,0,0,256,768)
-        weave_tokens(A,0)
-        gather(0,0)
-        cast_x(A,1,0)
-        load_x(3,0)
-        cast_x(A,3,0)
-        load_x(2,0)
-        weave_slots(V,0)
-        load_x(2,1)
-        cast_x(V,1,1,0,896)
+        cast_x(V,0,0,0,512)
+        load_x(1,1)
+        load_x(1,0)
+        cast_x(V,0,0,512,768)
+        cast_x(A,0,0,768,1280)
+        weave_tokens(V,0)
         load_w(6,(0,2,4))
-        quant_tokens(0)
+        cast_w(GP,6,0,2)
         load_x(3,1)
-        load_w(0)
-        cast_x(V,1,1,896,1280)
-        gather(1,1)
-        quant_slots(0)
-        load_w(1)
-        gather(1,0)
-        load_w(2)
-        gather(3,0)
-        cast_x(A,2,0)
+        load_x(2,1)
+        cast_x(A,1,1)
+        load_x(2,0)
+        load_x(3,0)
+        cast_x(A,1,0)
+        gather(0,0)
+        weave_slots(A,0)
+        weave_tokens(A,1)
+        load_w(1,(0,2,4))
+        quant_tokens(0)
         cast_x(A,2,1)
-        weave_tokens(V,1)
-        weave_slots(A,1)
-        quant_tokens(1)
-        weave_tokens(A,2)
-        cast_w(V,6,0,2)
-        cast_w(V,6,2,4)
-        quant_w(6,2,4)
-        gather(2,0)
-        quant_slots(1)
-        load_w(4)
-        cast_x(A,3,1)
-        cast_w(V,0)
-        gather(2,1)
-        gather(3,1)
+        gather(1,1)
+        gather(1,0)
+        cast_w(GP,6,2,4)
         quant_w(6,0,2)
-        quant_w(0)
-        mm_shared(0)
-        cast_w(A,1)
-        mm_shared(1)
-        quant_w(1)
-        cast_w(V,2)
-        load_w(5)
-        quant_tokens(2)
+        cast_x(A,2,0,0,1024)
+        cast_x(A,3,0)
+        weave_slots(V,1)
+        cast_w(A,1,2,4)
+        load_w(5,(0,2,4))
+        quant_w(6,2,4)
+        cast_w(GP,1,0,2)
+        load_w(4,(0,2,4))
+        load_w(0,(0,2,4))
+        load_w(2)
+        quant_slots(1)
+        cast_x(V,3,1)
+        quant_slots(0)
+        gather(3,1)
+        cast_x(V,2,0,1024,1280)
+        quant_tokens(1)
+        cast_w(GP,5,0,2)
+        gather(2,0)
+        gather(3,0)
+        gather(2,1)
+        weave_tokens(A,2)
         weave_slots(A,3)
+        cast_w(GP,5,2,4)
+        quant_w(1)
+        mm_shared(0)
+        mm_shared(1)
+        quant_w(5)
+        weave_slots(A,2)
+        cast_w(V,4)
         quant_slots(3)
         weave_tokens(A,3)
-        mm_shared(2)
-        nc.sync.dma_start(gates[:], gate)
-        cast_w(V,5)
-        quant_tokens(3)
-        mm_shared(3)
-        load_w(3)
-        cast_w(A,4)
-        weave_slots(A,2)
+        cast_w(A,2)
         quant_w(4)
         quant_slots(2)
-        quant_w(5)
-        mm_routed(0)
-        mm_routed(4)
+        load_w(3,(0,2,4))
+        cast_w(V,0)
+        quant_tokens(2)
         cast_w(A,3)
-        quant_w(2)
-        mm_routed(5)
-        quant_w(3)
-        mm_routed(2)
-        ycopy(A,4,6)
+        quant_w(0)
+        mm_routed(4)
         mm_routed(1)
-        scatter(512,768)
+        mm_routed(5)
+        quant_tokens(3)
+        mm_shared(2)
+        quant_w(2)
+        ycopy(A,4,6)
+        quant_w(3)
+        mm_routed(0)
+        mm_routed(2)
         mm_routed(3)
         ycopy(A,0,4)
+        nc.sync.dma_start(gates[:], gate)
+        scatter(512,768)
         scatter(0,512)
+        mm_shared(3)
         for bank, (a, b) in zip(shared, BANKS):
             nc.vector.tensor_tensor(result[:, a:b], bank[:], window[:, a:b], ADD)
             nc.sync.dma_start(out[:, a:b], result[:, a:b])

@@ -26,12 +26,13 @@ def tile_moe_shr_lin_none_kernel(tc, xT, w, gate, offs, out):
     nc = tc.nc
     with ExitStack() as ctx:
         keep = ctx.enter_context(tc.tile_pool(name="keep", bufs=1))
-        xraw_pool = ctx.enter_context(tc.tile_pool(name="xraw", bufs=4))
+        xraw_pool = ctx.enter_context(tc.tile_pool(name="xraw", bufs=3))
         wraw_pool = ctx.enter_context(tc.tile_pool(name="wraw", bufs=3))
-        pair_pool = ctx.enter_context(tc.tile_pool(name="pairs", bufs=3))
-        ring = ctx.enter_context(tc.tile_pool(name="ring", bufs=2))
-        quad_pool = ctx.enter_context(tc.tile_pool(name="quadp", bufs=3))
-        wring = ctx.enter_context(tc.tile_pool(name="wring", bufs=4))
+        pair_pool = ctx.enter_context(tc.tile_pool(name="pairs", bufs=2))
+        gp_pool = ctx.enter_context(tc.tile_pool(name="gpp", bufs=5))
+        gq_pool = ctx.enter_context(tc.tile_pool(name="gqp", bufs=2))
+        quad_pool = ctx.enter_context(tc.tile_pool(name="quadp", bufs=2))
+        wring = ctx.enter_context(tc.tile_pool(name="wring", bufs=7))
         psum = ctx.enter_context(tc.psum_pool(name="psum", bufs=1))
 
         offsets = keep.tile([P, S // 16], U16, name="offsets")
@@ -107,7 +108,7 @@ def tile_moe_shr_lin_none_kernel(tc, xT, w, gate, offs, out):
 
         def gather(g, u):
             if g not in gp:
-                gp[g] = ring.tile([P, 2, 2 * S], BF16, name="gp", align_bytes=64)
+                gp[g] = gp_pool.tile([P, 2, 2 * S], BF16, name="gp", align_bytes=64)
             nc.vector.tensor_copy(gp[g][:, u, :].bitcast(U32), pairs[g][:, u, :].bitcast(U32).indirect(offsets[:]))
 
         def weave_tokens(engine_copy, g):
@@ -115,7 +116,7 @@ def tile_moe_shr_lin_none_kernel(tc, xT, w, gate, offs, out):
             weave(engine_copy, quads[g][:], pairs[g][:])
 
         def weave_slots(engine_copy, g):
-            gq[g] = ring.tile([P, 4 * S], BF16, name="gq", align_bytes=64)
+            gq[g] = gq_pool.tile([P, 4 * S], BF16, name="gq", align_bytes=64)
             weave(engine_copy, gq[g][:], gp[g][:])
 
         def quant_tokens(g):
@@ -166,86 +167,87 @@ def tile_moe_shr_lin_none_kernel(tc, xT, w, gate, offs, out):
 
         H = T // 2
 
-        load_x(0,1)
-        load_x(0,0)
-        cast_x(V,0,1)
-        gather(0,1)
-        cast_x(V,0,0,0,512)
-        load_x(1,1)
-        load_x(1,0)
-        cast_x(V,0,0,512,768)
-        cast_x(A,0,0,768,1280)
-        weave_tokens(V,0)
-        load_w(6,(0,2,4))
-        cast_w(GP,6,0,2)
-        load_x(3,1)
-        load_x(2,1)
-        cast_x(A,1,1)
-        load_x(2,0)
         load_x(3,0)
-        cast_x(A,1,0)
-        gather(0,0)
-        weave_slots(A,0)
-        weave_tokens(A,1)
-        load_w(1,(0,2,4))
-        quant_tokens(0)
-        cast_x(A,2,1)
-        gather(1,1)
-        gather(1,0)
-        cast_w(GP,6,2,4)
-        quant_w(6,0,2)
-        cast_x(A,2,0,0,1024)
-        cast_x(A,3,0)
-        weave_slots(V,1)
-        cast_w(A,1,2,4)
-        load_w(5,(0,2,4))
-        quant_w(6,2,4)
-        cast_w(GP,1,0,2)
-        load_w(4,(0,2,4))
-        load_w(0,(0,2,4))
-        load_w(2)
-        quant_slots(1)
-        cast_x(V,3,1)
-        quant_slots(0)
+        load_x(3,1,(0,640,1280))
+        cast_x(A,3,1,640,896)
+        load_x(1,1,(0,512,896,1280))
+        cast_x(V,3,1,896,1280)
+        cast_x(V,3,0)
+        cast_x(A,3,1,0,384)
+        load_x(0,0)
+        cast_x(A,3,1,384,640)
+        load_x(1,0)
         gather(3,1)
-        cast_x(V,2,0,1024,1280)
-        quant_tokens(1)
-        cast_w(GP,5,0,2)
-        gather(2,0)
-        gather(3,0)
-        gather(2,1)
-        weave_tokens(A,2)
-        weave_slots(A,3)
-        cast_w(GP,5,2,4)
-        quant_w(1)
-        mm_shared(0)
-        mm_shared(1)
-        quant_w(5)
-        weave_slots(A,2)
-        cast_w(V,4)
-        quant_slots(3)
-        weave_tokens(A,3)
-        cast_w(A,2)
-        quant_w(4)
-        quant_slots(2)
+        weave_tokens(V,3)
         load_w(3,(0,2,4))
-        cast_w(V,0)
-        quant_tokens(2)
-        cast_w(A,3)
-        quant_w(0)
-        mm_routed(4)
-        mm_routed(1)
-        mm_routed(5)
+        cast_x(A,1,1,0,512)
+        cast_w(GP,3,0,2)
+        cast_x(A,1,1,512,1280)
+        cast_w(GP,3,2,4)
+        cast_x(A,1,0)
+        load_x(0,1)
+        gather(3,0)
         quant_tokens(3)
-        mm_shared(2)
+        load_w(6,(0,2,4))
+        weave_tokens(A,1)
+        cast_x(A,0,0)
+        load_x(2,0)
+        weave_slots(V,3)
+        cast_x(V,0,1)
+        gather(1,1)
+        cast_w(A,6)
+        load_x(2,1)
+        load_w(5,(0,2,4))
+        weave_tokens(V,0)
+        gather(1,0)
+        quant_tokens(1)
+        cast_x(A,2,0)
+        cast_w(GP,5,2,4)
+        weave_slots(A,1)
+        load_w(0,(0,2,4))
+        cast_w(A,5,0,2)
+        cast_w(GP,0,0,2)
+        cast_x(A,2,1)
+        quant_tokens(0)
+        gather(0,0)
+        quant_w(6)
+        quant_slots(3)
+        cast_w(GP,0,2,4)
+        load_w(2,(0,2,4))
+        quant_w(5)
+        load_w(4)
+        load_w(1,(0,2,4))
+        weave_tokens(A,2)
+        gather(2,1)
+        quant_slots(1)
+        gather(2,0)
+        cast_w(A,4)
+        gather(0,1)
+        weave_slots(A,2)
+        quant_slots(2)
+        quant_w(0)
+        cast_w(V,1,0,2)
+        weave_slots(A,0)
+        quant_slots(0)
+        cast_w(V,2)
+        cast_w(A,1,2,4)
+        mm_routed(5)
+        mm_shared(0)
         quant_w(2)
-        ycopy(A,4,6)
         quant_w(3)
-        mm_routed(0)
-        mm_routed(2)
+        quant_w(4)
         mm_routed(3)
-        ycopy(A,0,4)
+        mm_routed(4)
         nc.sync.dma_start(gates[:], gate)
+        mm_routed(0)
+        ycopy(A,4,6)
+        quant_w(1)
+        mm_routed(2)
+        mm_shared(1)
+        mm_routed(1)
+        quant_tokens(2)
+        mm_shared(2)
+        ycopy(A,0,4)
         scatter(512,768)
         scatter(0,512)
         mm_shared(3)

from contextlib import ExitStack

import concourse.mybir as mybir

K, T, E, C, N = 2048, 1280, 6, 128, 128
S = E * C

FLOPS = 2 * K * N * (S + T)

F32 = mybir.dt.float32
BF16 = mybir.dt.bfloat16
U32 = mybir.dt.uint32
U16 = mybir.dt.uint16
U8 = mybir.dt.uint8
FP8X4 = mybir.dt.float8_e4m3fn_x4
ADD = mybir.AluOpType.add
MULT = mybir.AluOpType.mult

P = 128
KP = 512
G = K // KP
BANKS = ((0, 512), (512, 1024), (1024, 1280))


def tile_moe_shr_lin_none_kernel(tc, xT, w, gate, offs, out):
    nc = tc.nc
    with ExitStack() as ctx:
        keep = ctx.enter_context(tc.tile_pool(name="keep", bufs=1))
        xraw_pool = ctx.enter_context(tc.tile_pool(name="xraw", bufs=3))
        wraw_pool = ctx.enter_context(tc.tile_pool(name="wraw", bufs=3))
        pair_pool = ctx.enter_context(tc.tile_pool(name="pairs", bufs=2))
        gp_pool = ctx.enter_context(tc.tile_pool(name="gpp", bufs=5))
        gq_pool = ctx.enter_context(tc.tile_pool(name="gqp", bufs=2))
        quad_pool = ctx.enter_context(tc.tile_pool(name="quadp", bufs=2))
        wring = ctx.enter_context(tc.tile_pool(name="wring", bufs=7))
        psum = ctx.enter_context(tc.psum_pool(name="psum", bufs=1))

        offsets = keep.tile([P, S // 16], U16, name="offsets")
        nc.sync.dma_start(offsets[:], offs)

        xc = keep.tile([P, G, T], U32, name="xc", align_bytes=64)
        xs = keep.tile([P, G, T], U8, name="xs", align_bytes=64)
        gc = keep.tile([P, G, S], U32, name="gc", align_bytes=64)
        gs = keep.tile([P, G, S], U8, name="gs", align_bytes=64)
        wc = keep.tile([P, E + 1, KP], U32, name="wc", align_bytes=64)
        ws = keep.tile([P, E + 1, KP], U8, name="ws", align_bytes=64)
        window = keep.tile([P, T], F32, name="window")
        result = keep.tile([P, T], F32, name="result")
        gates = keep.tile([P, S], F32, name="gates")
        y = keep.tile([P, S], F32, name="y")
        nc.gpsimd.memset(window[:], 0.0)

        shared = [psum.tile([P, b - a], F32, name=f"shared{a}") for a, b in BANKS]
        routed = [psum.tile([P, 512], F32, name="routed0"), psum.tile([P, 256], F32, name="routed1")]

        raws, pairs, wraws, wquads = {}, {}, {}, {}

        def load_x(g, u, cuts=(0, T)):
            raw = xraw_pool.tile([P, 2, T], F32, name="xraw")
            src = xT[g * KP : (g + 1) * KP, :].rearrange("(p u e) t -> p u e t", u=2, e=2)
            for a, b in zip(cuts[:-1], cuts[1:]):
                nc.sync.dma_start(raw[:, :, a:b], src[:, u, :, a:b])
            raws[g, u] = raw

        def load_w(e, cuts=(0, G)):
            raw = wraw_pool.tile([P, G, KP], F32, name="wraw")
            src = w[e].rearrange("(g p j) n -> p g (j n)", p=P, j=4)
            for a, b in zip(cuts[:-1], cuts[1:]):
                nc.sync.dma_start(raw[:, a:b, :], src[:, a:b, :])
            wraws[e] = raw

        def cast_x(engine_copy, g, u, a=0, b=T):
            if g not in pairs:
                pairs[g] = pair_pool.tile([P, 2, 2 * T], BF16, name="pairs", align_bytes=64)
            engine_copy(
                out=pairs[g][:, u, :].rearrange("p (t e) -> p t e", e=2)[:, a:b, :],
                in_=raws[g, u][:, :, a:b].rearrange("p e t -> p t e"),
            )

        def cast_w(engine_copy, e, a=0, b=G):
            if e not in wquads:
                wquads[e] = wring.tile([P, G, KP], BF16, name="wquad", align_bytes=64)
            if engine_copy is GP:
                GP(
                    wquads[e][:, a:b, :].rearrange("p g (n j) -> p g n j", j=4),
                    wraws[e][:, a:b, :].rearrange("p g (j n) -> p g n j", j=4),
                )
                return
            engine_copy(
                out=wquads[e][:, a:b, :].rearrange("p g (c i j) -> p g c j i", i=4, j=4),
                in_=wraws[e][:, a:b, :].rearrange("p g (j c i) -> p g c j i", i=4, j=4),
            )

        def quant_w(e, a=0, b=G):
            nc.vector.quantize_mx(
                out=wc[:, e, a * N : b * N].bitcast(FP8X4),
                scales=ws[:, e, a * N : b * N],
                in_=wquads[e][:, a:b, :].rearrange("p g c -> p (g c)"),
            )

        gp, gq, quads = {}, {}, {}

        def weave(engine_copy, dst, src):
            engine_copy(
                out=dst.bitcast(F32).rearrange("p (t u) -> p t u", u=2),
                in_=src.bitcast(F32).rearrange("p u t -> p t u"),
            )

        def gather(g, u):
            if g not in gp:
                gp[g] = gp_pool.tile([P, 2, 2 * S], BF16, name="gp", align_bytes=64)
            nc.vector.tensor_copy(gp[g][:, u, :].bitcast(U32), pairs[g][:, u, :].bitcast(U32).indirect(offsets[:]))

        def weave_tokens(engine_copy, g):
            quads[g] = quad_pool.tile([P, 4 * T], BF16, name="quads", align_bytes=64)
            weave(engine_copy, quads[g][:], pairs[g][:])

        def weave_slots(engine_copy, g):
            gq[g] = gq_pool.tile([P, 4 * S], BF16, name="gq", align_bytes=64)
            weave(engine_copy, gq[g][:], gp[g][:])

        def quant_tokens(g):
            for a, b in ((0, 1024), (1024, 1280)):
                nc.vector.quantize_mx(out=xc[:, g, a:b].bitcast(FP8X4), scales=xs[:, g, a:b], in_=quads[g][:, 4 * a : 4 * b])

        def quant_slots(g):
            for a, b in ((0, 512), (512, 768)):
                nc.vector.quantize_mx(out=gc[:, g, a:b].bitcast(FP8X4), scales=gs[:, g, a:b], in_=gq[g][:, 4 * a : 4 * b])

        def mm_shared(g):
            for bank, (a, b) in zip(shared, BANKS):
                nc.tensor.matmul_mx(
                    out=bank[:],
                    lhsT=wc[:, E, g * N : (g + 1) * N].bitcast(FP8X4),
                    lhsT_scale=ws[:, E, g * N : (g + 1) * N],
                    rhs=xc[:, g, a:b].bitcast(FP8X4),
                    rhs_scale=xs[:, g, a:b],
                    start=(g == 0),
                    stop=(g == G - 1),
                )

        def mm_routed(e):
            bank = routed[e // 4][:, (e % 4) * C : (e % 4 + 1) * C]
            for g in range(G):
                nc.tensor.matmul_mx(
                    out=bank,
                    lhsT=wc[:, e, g * N : (g + 1) * N].bitcast(FP8X4),
                    lhsT_scale=ws[:, e, g * N : (g + 1) * N],
                    rhs=gc[:, g, e * C : (e + 1) * C].bitcast(FP8X4),
                    rhs_scale=gs[:, g, e * C : (e + 1) * C],
                    start=(g == 0),
                    stop=(g == G - 1),
                )

        def ycopy(engine_copy, lo, hi):
            engine_copy(out=y[:, lo * C : hi * C], in_=routed[lo // 4][:, 0 : (hi - lo) * C])

        def scatter(a, b):
            nc.vector.tensor_tensor(
                window[:].indirect(offsets[:, a // 16 : b // 16]), y[:, a:b], gates[:, a:b], MULT
            )

        V, A = nc.vector.tensor_copy, nc.scalar.copy

        def GP(out, in_):
            nc.gpsimd.tensor_scalar(out, in_, 1.0, 0.0, MULT, ADD)

        H = T // 2

        load_x(3,0)
        load_x(3,1,(0,640,1280))
        cast_x(A,3,1,640,896)
        load_x(1,1,(0,512,896,1280))
        cast_x(V,3,1,896,1280)
        cast_x(V,3,0)
        cast_x(A,3,1,0,384)
        load_x(0,0)
        cast_x(A,3,1,384,640)
        load_x(1,0)
        gather(3,1)
        weave_tokens(V,3)
        load_w(3,(0,2,4))
        cast_x(A,1,1,0,512)
        cast_w(GP,3,0,2)
        cast_x(A,1,1,512,1280)
        cast_w(GP,3,2,4)
        cast_x(A,1,0)
        load_x(0,1)
        gather(3,0)
        quant_tokens(3)
        load_w(6,(0,2,4))
        weave_tokens(A,1)
        cast_x(A,0,0)
        load_x(2,0)
        weave_slots(V,3)
        cast_x(V,0,1)
        gather(1,1)
        cast_w(A,6)
        load_x(2,1)
        load_w(5,(0,2,4))
        weave_tokens(V,0)
        gather(1,0)
        quant_tokens(1)
        cast_x(A,2,0)
        cast_w(GP,5,2,4)
        weave_slots(A,1)
        load_w(0,(0,2,4))
        cast_w(A,5,0,2)
        cast_w(GP,0,0,2)
        cast_x(A,2,1)
        quant_tokens(0)
        gather(0,0)
        quant_w(6)
        quant_slots(3)
        cast_w(GP,0,2,4)
        load_w(2,(0,2,4))
        quant_w(5)
        load_w(4)
        load_w(1,(0,2,4))
        weave_tokens(A,2)
        gather(2,1)
        quant_slots(1)
        gather(2,0)
        cast_w(A,4)
        gather(0,1)
        weave_slots(A,2)
        quant_slots(2)
        quant_w(0)
        cast_w(V,1,0,2)
        weave_slots(A,0)
        quant_slots(0)
        cast_w(V,2)
        cast_w(A,1,2,4)
        mm_routed(5)
        mm_shared(0)
        quant_w(2)
        quant_w(3)
        quant_w(4)
        mm_routed(3)
        mm_routed(4)
        nc.sync.dma_start(gates[:], gate)
        mm_routed(0)
        ycopy(A,4,6)
        quant_w(1)
        mm_routed(2)
        mm_shared(1)
        mm_routed(1)
        quant_tokens(2)
        mm_shared(2)
        ycopy(A,0,4)
        scatter(512,768)
        scatter(0,512)
        mm_shared(3)
        for bank, (a, b) in zip(shared, BANKS):
            nc.vector.tensor_tensor(result[:, a:b], bank[:], window[:, a:b], ADD)
            nc.sync.dma_start(out[:, a:b], result[:, a:b])
